import numpy as np
import ml_dtypes


def mxq(x, axis, fmt="e4m3"):
    dtype, down = {"e4m3": (ml_dtypes.float8_e4m3fn, 7), "e5m2": (ml_dtypes.float8_e5m2, 14)}[fmt]
    v = np.moveaxis(np.asarray(x, np.float32).astype(ml_dtypes.bfloat16).astype(np.float64), axis, -1)
    blocks = v.reshape(v.shape[:-1] + (-1, 32))
    amax = np.abs(blocks).max(-1, keepdims=True)
    byte = np.maximum(np.where(amax > 0, np.frexp(amax)[1] - 1 + 127, 0) - down, 1)
    scale = np.exp2(byte - 127.0)
    codes = (blocks / scale).astype(np.float32).astype(dtype).astype(np.float64)
    return np.moveaxis((codes * scale).reshape(v.shape), -1, axis)


WIDE = False


def mx_kscale(k):
    if not WIDE:
        return np.ones(k)
    levels = np.array([10, -10, 5, -5, 0])
    if k % 512:
        return np.exp2(np.random.permutation(np.resize(levels, k // 32))).repeat(32)
    a = np.empty((k // 512, 16))
    for p in range(k // 512):
        a[p, :8] = np.random.permutation(np.resize(levels, 8))
        for g in range(8):
            far = levels[np.abs(levels - a[p, g]) >= 10]
            a[p, g + 8] = far[np.random.randint(len(far))]
    return np.exp2(a.ravel()).repeat(32)


def f64(x):
    return np.asarray(x).astype(np.float64)


E2M1 = np.array([0.0, 0.5, 1.0, 1.5, 2.0, 3.0, 4.0, 6.0, -0.0, -0.5, -1.0, -1.5, -2.0, -3.0, -4.0, -6.0])


def pack_weight(w, fmt):
    k, n = w.shape
    w = f64(np.asarray(w, np.float32).astype(ml_dtypes.bfloat16)).reshape(k // 32, 32, n)
    amax = np.abs(w).max(1)
    if fmt == "e4m3":
        byte = np.frexp(amax)[1] - 1 + 127 - 7
    else:
        mant, ex = np.frexp(amax / 6.0)
        byte = np.where(mant > 0.5, ex, ex - 1) + 127
    byte = np.clip(np.where(amax > 0, byte, 1), 1, 254)
    scaled = (w * np.exp2(127.0 - byte)[:, None, :]).reshape(k, n).astype(np.float32)
    by_word = np.ascontiguousarray(scaled.reshape(k // 512, 128, 4, n).transpose(0, 1, 3, 2))
    if fmt == "e4m3":
        words = by_word.astype(ml_dtypes.float8_e4m3fn).view(np.uint8)
    else:
        c = by_word.astype(ml_dtypes.float4_e2m1fn).view(np.uint8) & 0xF
        words = (c[..., 0::2] | (c[..., 1::2] << 4)).reshape(k // 512, 128, 2 * n)
    return np.ascontiguousarray(words), np.ascontiguousarray(byte.astype(np.uint8).reshape(k // 512, 16, n))


def unpack_weight(words, scales, fmt):
    g, _, n = scales.shape
    words = np.ascontiguousarray(words).reshape(g, 128, n, -1)
    if fmt == "e4m3":
        vals = words.view(ml_dtypes.float8_e4m3fn).astype(np.float64)
    else:
        nib = np.empty((g, 128, n, 4), np.uint8)
        nib[..., 0::2] = words & 0xF
        nib[..., 1::2] = words >> 4
        vals = E2M1[nib]
    vals = vals * np.repeat(np.exp2(scales.astype(np.float64) - 127.0), 8, axis=1)[..., None]
    return vals.transpose(0, 1, 3, 2).reshape(g * 512, n)


D, K, M, T = 512, 512, 1024, 1536


def setup_inputs():
    n = np.random.standard_normal
    s = mx_kscale(K)[:, None]
    p_w0 = pack_weight(n((K, M)) / np.sqrt(K) / s, "e2m1")
    p_w1 = pack_weight(n((K, M)) / np.sqrt(K) / s, "e4m3")
    return {
        "x": (n((K, T + 2 * D)) * s).astype(np.float32),
        "w0_words": p_w0[0],
        "w0_scales": p_w0[1],
        "w1_words": p_w1[0],
        "w1_scales": p_w1[1],
        "w2": (n((K, M)) / np.sqrt(K) / s).astype(np.float32),
    }


def reference(x, w0_words, w0_scales, w1_words, w1_scales, w2):
    x_ = mxq(f64(x), 0, "e4m3")
    w0_ = unpack_weight(w0_words, w0_scales, "e2m1")
    w1_ = unpack_weight(w1_words, w1_scales, "e4m3")
    w2_ = mxq(f64(w2), 0, "e4m3")
    y = x_[:, :T].T @ w0_ + x_[:, D:D + T].T @ w1_ + x_[:, 2 * D:].T @ w2_
    return y

@@ -1,0 +1,153 @@
+from contextlib import ExitStack
+
+import concourse.mybir as mybir
+
+D, K, M, T = 512, 512, 1024, 1536
+FLOPS = 2 * 3 * K * M * T
+
+F32 = mybir.dt.float32
+BF16 = mybir.dt.bfloat16
+I32 = mybir.dt.int32
+U32 = mybir.dt.uint32
+U8 = mybir.dt.uint8
+FP8X4 = mybir.dt.float8_e4m3fn_x4
+FP4X4 = mybir.dt.float4_e2m1fn_x4
+
+P = 128
+PACK = 4
+ROWS = 128
+COLS = 512
+TILES = D // ROWS
+HALVES = M // COLS
+
+
+def tile_mix_dconv_tm_none_kernel(tc, x, w0_words, w0_scales, w1_words, w1_scales, w2, out):
+    nc = tc.nc
+    with ExitStack() as ctx:
+        keep = ctx.enter_context(tc.tile_pool(name="keep", bufs=1))
+        psum = ctx.enter_context(tc.psum_pool(name="psum", bufs=1))
+        ctx.enter_context(tc.manual_schedule())
+
+        x_codes = keep.tile([P, T + 2 * D], U32, align_bytes=64)
+        x_plane = keep.tile([P, T + 2 * D], U8, align_bytes=64)
+        w2_codes = keep.tile([P, M], U32, align_bytes=64)
+        w2_plane = keep.tile([P, M], U8, align_bytes=64)
+        w1_codes = keep.tile([P, M], U32, align_bytes=64)
+        w0_codes = keep.tile([P, 2 * M], U8, align_bytes=64)
+        w_planes = keep.tile([P, 2 * M], U8, align_bytes=64)
+        banks = [[psum.tile([ROWS, COLS], F32, name=f"bank_{i}_{h}") for h in range(HALVES)] for i in range(TILES)]
+        results = [keep.tile([ROWS, M], F32, name=f"result_{n}") for n in range(T // ROWS)]
+
+        def load_rows(name, source, first, width):
+            raw = keep.tile([P, PACK, width], F32, name=f"raw_{name}_{first}")
+            nc.sync.dma_start(out=raw[:], in_=source[:, first : first + width].rearrange("(p j) w -> p j w", j=PACK))
+            return raw
+
+        def load_scales(scales, first):
+            for r in range(4):
+                nc.sync.dma_start(
+                    out=w_planes[r:P:32, first : first + M].bitcast(I32), in_=scales[0, r:16:4, :].bitcast(I32)
+                )
+
+        def quantise(name, raw, codes, plane, first, with_scalar):
+            half = raw.shape[2] // 2
+            grouped = []
+            for u in range(2):
+                g = keep.tile([P, half, PACK], BF16, name=f"grouped_{name}_{first}_{u}", align_bytes=64)
+                copy = nc.scalar.copy if with_scalar and u == 1 else nc.vector.tensor_copy
+                copy(
+                    out=g[:].rearrange("p (c i) j -> p c j i", i=4),
+                    in_=raw[:, :, u * half : (u + 1) * half].rearrange("p j (c i) -> p c j i", i=4),
+                )
+                grouped.append(g)
+            for u in range(2):
+                cols = slice(first + u * half, first + (u + 1) * half)
+                nc.vector.quantize_mx(
+                    out=codes[:, cols].bitcast(FP8X4),
+                    scales=plane[:, cols],
+                    in_=grouped[u][:].rearrange("p w j -> p (w j)"),
+                )
+
+        def tap_pass(block, i, h, tap, start, stop):
+            t0 = (block + tap) * D + i * ROWS
+            n0 = h * COLS
+            if tap == 0:
+                rhs = w0_codes[:, 2 * n0 : 2 * (n0 + COLS)].bitcast(FP4X4)
+                rhs_scale = w_planes[:, n0 : n0 + COLS]
+            elif tap == 1:
+                rhs = w1_codes[:, n0 : n0 + COLS].bitcast(FP8X4)
+                rhs_scale = w_planes[:, M + n0 : M + n0 + COLS]
+            else:
+                rhs = w2_codes[:, n0 : n0 + COLS].bitcast(FP8X4)
+                rhs_scale = w2_plane[:, n0 : n0 + COLS]
+            nc.tensor.matmul_mx(
+                out=banks[i][h][:],
+                lhsT=x_codes[:, t0 : t0 + ROWS].bitcast(FP8X4),
+                lhsT_scale=x_plane[:, t0 : t0 + ROWS],
+                rhs=rhs,
+                rhs_scale=rhs_scale,
+                start=start,
+                stop=stop,
+            )
+
+        def drain(block, i, h, copy):
+            copy(out=results[block * TILES + i][:, h * COLS : (h + 1) * COLS], in_=banks[i][h][:])
+
+        def store(block, i):
+            n = block * TILES + i
+            nc.sync.dma_start(out=out[n * ROWS : (n + 1) * ROWS, :], in_=results[n][:])
+
+        nc.vector.memset(w_planes[:].bitcast(I32), 0)
+
+        raw_x1 = load_rows("x", x, D, D)
+        nc.sync.dma_start(out=w1_codes[:].bitcast(I32), in_=w1_words[0].rearrange("p n t -> p (n t)").bitcast(I32))
+        load_scales(w1_scales, M)
+        nc.sync.dma_start(out=w0_codes[:].bitcast(I32), in_=w0_words[0].bitcast(I32))
+        raw_x0 = load_rows("x", x, 0, D)
+        load_scales(w0_scales, 0)
+        raw_w2a = load_rows("w2", w2, 0, COLS)
+        raw_x2 = [load_rows("x", x, 2 * D + u * (D // 2), D // 2) for u in range(2)]
+        raw_w2b = load_rows("w2", w2, COLS, COLS)
+        raw_x3 = load_rows("x", x, 3 * D, D)
+        raw_x4 = load_rows("x", x, 4 * D, D)
+
+        quantise("x", raw_x1, x_codes, x_plane, D, True)
+        for i in range(TILES):
+            for h in range(HALVES):
+                tap_pass(0, i, h, 1, True, False)
+        quantise("x", raw_x0, x_codes, x_plane, 0, True)
+        for i in range(TILES):
+            for h in range(HALVES):
+                tap_pass(0, i, h, 0, False, False)
+        quantise("w2", raw_w2a, w2_codes, w2_plane, 0, True)
+        for u in range(2):
+            quantise("x", raw_x2[u], x_codes, x_plane, 2 * D + u * (D // 2), True)
+            pair = (2 * u, 2 * u + 1)
+            for i in pair:
+                tap_pass(0, i, 0, 2, False, True)
+                drain(0, i, 0, nc.scalar.copy)
+            for i in pair:
+                tap_pass(1, i, 0, 0, True, False)
+                tap_pass(1, i, 0, 1, False, False)
+        quantise("w2", raw_w2b, w2_codes, w2_plane, COLS, False)
+        for i in range(TILES):
+            tap_pass(0, i, 1, 2, False, True)
+            drain(0, i, 1, nc.scalar.copy)
+            store(0, i)
+        for i in range(TILES):
+            tap_pass(1, i, 1, 0, True, False)
+            tap_pass(1, i, 1, 1, False, False)
+        quantise("x", raw_x3, x_codes, x_plane, 3 * D, False)
+        for i in range(TILES):
+            for h in range(HALVES):
+                tap_pass(1, i, h, 2, False, True)
+                drain(1, i, h, nc.scalar.copy)
+            store(1, i)
+        quantise("x", raw_x4, x_codes, x_plane, 4 * D, False)
+        for i in range(TILES):
+            for tap in range(3):
+                for h in range(HALVES):
+                    tap_pass(2, i, h, tap, tap == 0, tap == 2)
+            drain(2, i, 0, nc.scalar.copy)
+            drain(2, i, 1, nc.vector.tensor_copy)
+            store(2, i)

@@ -17,8 +17,9 @@ P = 128
 PACK = 4
 ROWS = 128
 COLS = 512
-TILES = D // ROWS
-HALVES = M // COLS
+CHUNK = 256
+TILES = CHUNK // ROWS
+TAPS = 3
 
 
 def tile_mix_dconv_tm_none_kernel(tc, x, w0_words, w0_scales, w1_words, w1_scales, w2, out):
@@ -33,9 +34,10 @@ def tile_mix_dconv_tm_none_kernel(tc, x, w0_words, w0_scales, w1_words, w1_scale
         w2_codes = keep.tile([P, M], U32, align_bytes=64)
         w2_plane = keep.tile([P, M], U8, align_bytes=64)
         w1_codes = keep.tile([P, M], U32, align_bytes=64)
+        w1_plane = keep.tile([P, M], U8, align_bytes=64)
         w0_codes = keep.tile([P, 2 * M], U8, align_bytes=64)
-        w_planes = keep.tile([P, 2 * M], U8, align_bytes=64)
-        banks = [[psum.tile([ROWS, COLS], F32, name=f"bank_{i}_{h}") for h in range(HALVES)] for i in range(TILES)]
+        w0_plane = keep.tile([P, M], U8, align_bytes=64)
+        banks = [[psum.tile([ROWS, COLS], F32, name=f"bank_{s}_{i}") for i in range(TILES)] for s in range(4)]
         results = [keep.tile([ROWS, M], F32, name=f"result_{n}") for n in range(T // ROWS)]
 
         def load_rows(name, source, first, width):
@@ -43,111 +45,139 @@ def tile_mix_dconv_tm_none_kernel(tc, x, w0_words, w0_scales, w1_words, w1_scale
             nc.sync.dma_start(out=raw[:], in_=source[:, first : first + width].rearrange("(p j) w -> p j w", j=PACK))
             return raw
 
-        def load_scales(scales, first):
+        def load_scales(queue, scales, plane):
             for r in range(4):
-                nc.sync.dma_start(
-                    out=w_planes[r:P:32, first : first + M].bitcast(I32), in_=scales[0, r:16:4, :].bitcast(I32)
-                )
+                queue.dma_start(out=plane[r:P:32, :].bitcast(I32), in_=scales[0, r:16:4, :].bitcast(I32))
 
-        def quantise(name, raw, codes, plane, first, with_scalar):
-            half = raw.shape[2] // 2
+        def quantise(name, raw, codes, plane, first, pieces):
             grouped = []
-            for u in range(2):
-                g = keep.tile([P, half, PACK], BF16, name=f"grouped_{name}_{first}_{u}", align_bytes=64)
-                copy = nc.scalar.copy if with_scalar and u == 1 else nc.vector.tensor_copy
+            for lo, hi, copy in pieces:
+                g = keep.tile([P, hi - lo, PACK], BF16, name=f"grouped_{name}_{first + lo}", align_bytes=64)
                 copy(
                     out=g[:].rearrange("p (c i) j -> p c j i", i=4),
-                    in_=raw[:, :, u * half : (u + 1) * half].rearrange("p j (c i) -> p c j i", i=4),
+                    in_=raw[:, :, lo:hi].rearrange("p j (c i) -> p c j i", i=4),
                 )
                 grouped.append(g)
-            for u in range(2):
-                cols = slice(first + u * half, first + (u + 1) * half)
+            for (lo, hi, copy), g in zip(pieces, grouped):
                 nc.vector.quantize_mx(
-                    out=codes[:, cols].bitcast(FP8X4),
-                    scales=plane[:, cols],
-                    in_=grouped[u][:].rearrange("p w j -> p (w j)"),
+                    out=codes[:, first + lo : first + hi].bitcast(FP8X4),
+                    scales=plane[:, first + lo : first + hi],
+                    in_=g[:].rearrange("p w j -> p (w j)"),
                 )
 
-        def tap_pass(block, i, h, tap, start, stop):
-            t0 = (block + tap) * D + i * ROWS
+        vec, sca = nc.vector.tensor_copy, nc.scalar.copy
+
+        def quantise_x(u, m, second):
+            quantise("x", raw_x[u][m], x_codes, x_plane, m * D + u * CHUNK, [(0, ROWS, vec), (ROWS, CHUNK, second)])
+
+        def quantise_w2(h):
+            quantise("w2", raw_w2[h], w2_codes, w2_plane, h * COLS, [(0, 256, vec), (256, 384, vec), (384, COLS, sca)])
+
+        def tap_pass(slot, u, r, h, tap, i):
+            t0 = (r + tap) * D + u * CHUNK + i * ROWS
             n0 = h * COLS
             if tap == 0:
                 rhs = w0_codes[:, 2 * n0 : 2 * (n0 + COLS)].bitcast(FP4X4)
-                rhs_scale = w_planes[:, n0 : n0 + COLS]
-            elif tap == 1:
-                rhs = w1_codes[:, n0 : n0 + COLS].bitcast(FP8X4)
-                rhs_scale = w_planes[:, M + n0 : M + n0 + COLS]
             else:
-                rhs = w2_codes[:, n0 : n0 + COLS].bitcast(FP8X4)
-                rhs_scale = w2_plane[:, n0 : n0 + COLS]
+                rhs = (w1_codes, w2_codes)[tap - 1][:, n0 : n0 + COLS].bitcast(FP8X4)
             nc.tensor.matmul_mx(
-                out=banks[i][h][:],
+                out=banks[slot][i][:],
                 lhsT=x_codes[:, t0 : t0 + ROWS].bitcast(FP8X4),
                 lhsT_scale=x_plane[:, t0 : t0 + ROWS],
                 rhs=rhs,
-                rhs_scale=rhs_scale,
-                start=start,
-                stop=stop,
+                rhs_scale=(w0_plane, w1_plane, w2_plane)[tap][:, n0 : n0 + COLS],
+                start=tap == 0,
+                stop=tap == TAPS - 1,
             )
 
-        def drain(block, i, h, copy):
-            copy(out=results[block * TILES + i][:, h * COLS : (h + 1) * COLS], in_=banks[i][h][:])
+        def result_of(u, r, i):
+            return (r * D + u * CHUNK) // ROWS + i
 
-        def store(block, i):
-            n = block * TILES + i
+        def drain(slot, u, r, h, i, copy):
+            copy(out=results[result_of(u, r, i)][:, h * COLS : (h + 1) * COLS], in_=banks[slot][i][:])
+
+        def store(u, r, i):
+            n = result_of(u, r, i)
             nc.sync.dma_start(out=out[n * ROWS : (n + 1) * ROWS, :], in_=results[n][:])
 
-        nc.vector.memset(w_planes[:].bitcast(I32), 0)
+        def open_taps(slot, u, r, h, taps):
+            for i in range(TILES):
+                for tap in taps:
+                    tap_pass(slot, u, r, h, tap, i)
 
-        raw_x1 = load_rows("x", x, D, D)
-        nc.sync.dma_start(out=w1_codes[:].bitcast(I32), in_=w1_words[0].rearrange("p n t -> p (n t)").bitcast(I32))
-        load_scales(w1_scales, M)
+        def close_half(slot, u, r, h):
+            for i in range(TILES):
+                tap_pass(slot, u, r, h, 2, i)
+                drain(slot, u, r, h, i, sca)
+
+        def both_halves(slots, u, r, tap):
+            for i in range(TILES):
+                for h in range(2):
+                    tap_pass(slots[h], u, r, h, tap, i)
+
+        def close_both(slots, u, r, second):
+            for i in range(TILES):
+                for h in range(2):
+                    tap_pass(slots[h], u, r, h, 2, i)
+                    drain(slots[h], u, r, h, i, (sca, second)[h])
+                store(u, r, i)
+
+        nc.vector.memset(w1_plane[:].bitcast(I32), 0)
+        nc.vector.memset(w0_plane[:].bitcast(I32), 0)
+
+
+        raw_x = [[], []]
+        raw_w2 = []
+        raw_x[0].append(load_rows("x", x, 0, CHUNK))
         nc.sync.dma_start(out=w0_codes[:].bitcast(I32), in_=w0_words[0].bitcast(I32))
-        raw_x0 = load_rows("x", x, 0, D)
-        load_scales(w0_scales, 0)
-        raw_w2a = load_rows("w2", w2, 0, COLS)
-        raw_x2 = [load_rows("x", x, 2 * D + u * (D // 2), D // 2) for u in range(2)]
-        raw_w2b = load_rows("w2", w2, COLS, COLS)
-        raw_x3 = load_rows("x", x, 3 * D, D)
-        raw_x4 = load_rows("x", x, 4 * D, D)
+        load_scales(nc.sync, w0_scales, w0_plane)
+        nc.sync.dma_start(out=w1_codes[:].bitcast(I32), in_=w1_words[0].rearrange("p n t -> p (n t)").bitcast(I32))
+        raw_x[0].append(load_rows("x", x, D, CHUNK))
+        load_scales(nc.sync, w1_scales, w1_plane)
+        raw_x[0].append(load_rows("x", x, 2 * D, CHUNK))
+        raw_w2.append(load_rows("w2", w2, 0, COLS))
+        raw_x[0].append(load_rows("x", x, 3 * D, CHUNK))
+        raw_w2.append(load_rows("w2", w2, COLS, COLS))
+        raw_x[0].append(load_rows("x", x, 4 * D, CHUNK))
+        for m in range(5):
+            raw_x[1].append(load_rows("x", x, m * D + CHUNK, CHUNK))
 
-        quantise("x", raw_x1, x_codes, x_plane, D, True)
+        quantise_x(0, 0, sca)
+        both_halves((0, 1), 0, 0, 0)
+        quantise_x(0, 1, sca)
+        both_halves((0, 1), 0, 0, 1)
+        both_halves((2, 3), 0, 1, 0)
+        quantise_x(0, 2, sca)
+        both_halves((2, 3), 0, 1, 1)
+        quantise_w2(0)
+        quantise_x(0, 3, sca)
+        close_half(0, 0, 0, 0)
+        close_half(2, 0, 1, 0)
+        open_taps(0, 0, 2, 0, (0, 1))
+        open_taps(2, 0, 2, 1, (0, 1))
+        quantise_w2(1)
+        for slot, r in ((1, 0), (3, 1)):
+            close_half(slot, 0, r, 1)
+            for i in range(TILES):
+                store(0, r, i)
+        quantise_x(0, 4, vec)
+        close_both((0, 2), 0, 2, sca)
+
+        quantise_x(1, 0, vec)
+        both_halves((1, 3), 1, 0, 0)
+        quantise_x(1, 1, vec)
+        both_halves((1, 3), 1, 0, 1)
+        both_halves((0, 2), 1, 1, 0)
+        quantise_x(1, 2, vec)
+        quantise_x(1, 3, vec)
+        quantise_x(1, 4, vec)
+        close_both((1, 3), 1, 0, vec)
+        both_halves((0, 2), 1, 1, 1)
+        close_both((0, 2), 1, 1, vec)
         for i in range(TILES):
-            for h in range(HALVES):
-                tap_pass(0, i, h, 1, True, False)
-        quantise("x", raw_x0, x_codes, x_plane, 0, True)
-        for i in range(TILES):
-            for h in range(HALVES):
-                tap_pass(0, i, h, 0, False, False)
-        quantise("w2", raw_w2a, w2_codes, w2_plane, 0, True)
-        for u in range(2):
-            quantise("x", raw_x2[u], x_codes, x_plane, 2 * D + u * (D // 2), True)
-            pair = (2 * u, 2 * u + 1)
-            for i in pair:
-                tap_pass(0, i, 0, 2, False, True)
-                drain(0, i, 0, nc.scalar.copy)
-            for i in pair:
-                tap_pass(1, i, 0, 0, True, False)
-                tap_pass(1, i, 0, 1, False, False)
-        quantise("w2", raw_w2b, w2_codes, w2_plane, COLS, False)
-        for i in range(TILES):
-            tap_pass(0, i, 1, 2, False, True)
-            drain(0, i, 1, nc.scalar.copy)
-            store(0, i)
-        for i in range(TILES):
-            tap_pass(1, i, 1, 0, True, False)
-            tap_pass(1, i, 1, 1, False, False)
-        quantise("x", raw_x3, x_codes, x_plane, 3 * D, False)
-        for i in range(TILES):
-            for h in range(HALVES):
-                tap_pass(1, i, h, 2, False, True)
-                drain(1, i, h, nc.scalar.copy)
-            store(1, i)
-        quantise("x", raw_x4, x_codes, x_plane, 4 * D, False)
-        for i in range(TILES):
-            for tap in range(3):
-                for h in range(HALVES):
-                    tap_pass(2, i, h, tap, tap == 0, tap == 2)
-            drain(2, i, 0, nc.scalar.copy)
-            drain(2, i, 1, nc.vector.tensor_copy)
-            store(2, i)
+            for tap in range(TAPS):
+                for h in range(2):
+                    tap_pass((1, 3)[h], 1, 2, h, tap, i)
+            for h in range(2):
+                drain((1, 3)[h], 1, 2, h, i, (sca, vec)[h])
+            store(1, 2, i)

@@ -15,15 +15,22 @@ FP4X4 = mybir.dt.float4_e2m1fn_x4
 
 P = 128
 PACK = 4
+QUADRANT = 32
 ROWS = 128
 COLS = 512
 CHUNK = 256
 TILES = CHUNK // ROWS
+HALVES = M // COLS
 TAPS = 3
+SLOTS = 4
+RUN = 4
+PLANE_ROW = (0, 4, 0)
 
 
 def tile_mix_dconv_tm_none_kernel(tc, x, w0_words, w0_scales, w1_words, w1_scales, w2, out):
     nc = tc.nc
+    on_vector, on_scalar = nc.vector.tensor_copy, nc.scalar.copy
+
     with ExitStack() as ctx:
         keep = ctx.enter_context(tc.tile_pool(name="keep", bufs=1))
         psum = ctx.enter_context(tc.psum_pool(name="psum", bufs=1))
@@ -37,25 +44,33 @@ def tile_mix_dconv_tm_none_kernel(tc, x, w0_words, w0_scales, w1_words, w1_scale
         w1_plane = keep.tile([P, M], U8, align_bytes=64)
         w0_codes = keep.tile([P, 2 * M], U8, align_bytes=64)
         w0_plane = keep.tile([P, M], U8, align_bytes=64)
-        banks = [[psum.tile([ROWS, COLS], F32, name=f"bank_{s}_{i}") for i in range(TILES)] for s in range(4)]
+        banks = [[psum.tile([ROWS, COLS], F32, name=f"bank_{s}_{i}") for i in range(TILES)] for s in range(SLOTS)]
         results = [keep.tile([ROWS, M], F32, name=f"result_{n}") for n in range(T // ROWS)]
+        raw_x = {}
 
         def load_rows(name, source, first, width):
             raw = keep.tile([P, PACK, width], F32, name=f"raw_{name}_{first}")
             nc.sync.dma_start(out=raw[:], in_=source[:, first : first + width].rearrange("(p j) w -> p j w", j=PACK))
             return raw
 
-        def load_scales(queue, scales, plane):
+        def load_x(c, chunks):
+            raw = load_rows("x", x, c * CHUNK, chunks * CHUNK)
+            for u in range(chunks):
+                raw_x[c + u] = (raw, c * CHUNK)
+
+        def load_scales(scales, plane, first_row):
             for r in range(4):
-                queue.dma_start(out=plane[r:P:32, :].bitcast(I32), in_=scales[0, r:16:4, :].bitcast(I32))
+                nc.sync.dma_start(
+                    out=plane[first_row + r : P : QUADRANT, :].bitcast(I32), in_=scales[0, r:16:4, :].bitcast(I32)
+                )
 
         def quantise(name, raw, codes, plane, first, pieces):
             grouped = []
             for lo, hi, copy in pieces:
                 g = keep.tile([P, hi - lo, PACK], BF16, name=f"grouped_{name}_{first + lo}", align_bytes=64)
                 copy(
-                    out=g[:].rearrange("p (c i) j -> p c j i", i=4),
-                    in_=raw[:, :, lo:hi].rearrange("p j (c i) -> p c j i", i=4),
+                    out=g[:].rearrange("p (c i) j -> p c j i", i=RUN),
+                    in_=raw[:, :, lo:hi].rearrange("p j (c i) -> p c j i", i=RUN),
                 )
                 grouped.append(g)
             for (lo, hi, copy), g in zip(pieces, grouped):
@@ -65,16 +80,18 @@ def tile_mix_dconv_tm_none_kernel(tc, x, w0_words, w0_scales, w1_words, w1_scale
                     in_=g[:].rearrange("p w j -> p (w j)"),
                 )
 
-        vec, sca = nc.vector.tensor_copy, nc.scalar.copy
-
-        def quantise_x(u, m, second):
-            quantise("x", raw_x[u][m], x_codes, x_plane, m * D + u * CHUNK, [(0, ROWS, vec), (ROWS, CHUNK, second)])
+        def quantise_x(c, second_copy):
+            raw, first = raw_x[c]
+            lo = c * CHUNK - first
+            pieces = [(lo, lo + ROWS, on_vector), (lo + ROWS, lo + CHUNK, second_copy)]
+            quantise("x", raw, x_codes, x_plane, first, pieces)
 
         def quantise_w2(h):
-            quantise("w2", raw_w2[h], w2_codes, w2_plane, h * COLS, [(0, 256, vec), (256, 384, vec), (384, COLS, sca)])
+            pieces = [(0, 256, on_vector), (256, 384, on_vector), (384, COLS, on_scalar)]
+            quantise("w2", raw_w2[h], w2_codes, w2_plane, h * COLS, pieces)
 
-        def tap_pass(slot, u, r, h, tap, i):
-            t0 = (r + tap) * D + u * CHUNK + i * ROWS
+        def tap_pass(slot, c, h, tap, i):
+            t0 = c * CHUNK + tap * D + i * ROWS
             n0 = h * COLS
             if tap == 0:
                 rhs = w0_codes[:, 2 * n0 : 2 * (n0 + COLS)].bitcast(FP4X4)
@@ -85,99 +102,96 @@ def tile_mix_dconv_tm_none_kernel(tc, x, w0_words, w0_scales, w1_words, w1_scale
                 lhsT=x_codes[:, t0 : t0 + ROWS].bitcast(FP8X4),
                 lhsT_scale=x_plane[:, t0 : t0 + ROWS],
                 rhs=rhs,
-                rhs_scale=(w0_plane, w1_plane, w2_plane)[tap][:, n0 : n0 + COLS],
+                rhs_scale=(w0_plane, w1_plane, w2_plane)[tap][PLANE_ROW[tap] :, n0 : n0 + COLS],
                 start=tap == 0,
                 stop=tap == TAPS - 1,
             )
 
-        def result_of(u, r, i):
-            return (r * D + u * CHUNK) // ROWS + i
+        def drain(slot, c, h, i, copy):
+            copy(out=results[TILES * c + i][:, h * COLS : (h + 1) * COLS], in_=banks[slot][i][:])
 
-        def drain(slot, u, r, h, i, copy):
-            copy(out=results[result_of(u, r, i)][:, h * COLS : (h + 1) * COLS], in_=banks[slot][i][:])
-
-        def store(u, r, i):
-            n = result_of(u, r, i)
+        def store(c, i):
+            n = TILES * c + i
             nc.sync.dma_start(out=out[n * ROWS : (n + 1) * ROWS, :], in_=results[n][:])
 
-        def open_taps(slot, u, r, h, taps):
+        def one_tap(slots, c, tap):
             for i in range(TILES):
-                for tap in taps:
-                    tap_pass(slot, u, r, h, tap, i)
+                for h in range(HALVES):
+                    tap_pass(slots[h], c, h, tap, i)
 
-        def close_half(slot, u, r, h):
+        def open_half(slot, c, h):
             for i in range(TILES):
-                tap_pass(slot, u, r, h, 2, i)
-                drain(slot, u, r, h, i, sca)
+                for tap in range(TAPS - 1):
+                    tap_pass(slot, c, h, tap, i)
 
-        def both_halves(slots, u, r, tap):
+        def close_half(slot, c, h):
             for i in range(TILES):
-                for h in range(2):
-                    tap_pass(slots[h], u, r, h, tap, i)
+                tap_pass(slot, c, h, TAPS - 1, i)
+                drain(slot, c, h, i, on_scalar)
 
-        def close_both(slots, u, r, second):
+        def close_both(slots, c, second_copy):
             for i in range(TILES):
-                for h in range(2):
-                    tap_pass(slots[h], u, r, h, 2, i)
-                    drain(slots[h], u, r, h, i, (sca, second)[h])
-                store(u, r, i)
+                for h in range(HALVES):
+                    tap_pass(slots[h], c, h, TAPS - 1, i)
+                    drain(slots[h], c, h, i, (on_scalar, second_copy)[h])
+                store(c, i)
 
-        nc.vector.memset(w1_plane[:].bitcast(I32), 0)
         nc.vector.memset(w0_plane[:].bitcast(I32), 0)
+        nc.vector.memset(w1_plane[:].bitcast(I32), 0)
 
-
-        raw_x = [[], []]
-        raw_w2 = []
-        raw_x[0].append(load_rows("x", x, 0, CHUNK))
+        load_x(0, 1)
         nc.sync.dma_start(out=w0_codes[:].bitcast(I32), in_=w0_words[0].bitcast(I32))
-        load_scales(nc.sync, w0_scales, w0_plane)
+        load_scales(w0_scales, w0_plane, PLANE_ROW[0])
         nc.sync.dma_start(out=w1_codes[:].bitcast(I32), in_=w1_words[0].rearrange("p n t -> p (n t)").bitcast(I32))
-        raw_x[0].append(load_rows("x", x, D, CHUNK))
-        load_scales(nc.sync, w1_scales, w1_plane)
-        raw_x[0].append(load_rows("x", x, 2 * D, CHUNK))
-        raw_w2.append(load_rows("w2", w2, 0, COLS))
-        raw_x[0].append(load_rows("x", x, 3 * D, CHUNK))
+        load_x(2, 1)
+        load_x(4, 1)
+        load_scales(w1_scales, w1_plane, PLANE_ROW[1])
+        raw_w2 = [load_rows("w2", w2, 0, COLS)]
+        load_x(6, 2)
         raw_w2.append(load_rows("w2", w2, COLS, COLS))
-        raw_x[0].append(load_rows("x", x, 4 * D, CHUNK))
-        for m in range(5):
-            raw_x[1].append(load_rows("x", x, m * D + CHUNK, CHUNK))
+        load_x(8, 2)
+        for c in (1, 3, 5):
+            load_x(c, 1)
 
-        quantise_x(0, 0, sca)
-        both_halves((0, 1), 0, 0, 0)
-        quantise_x(0, 1, sca)
-        both_halves((0, 1), 0, 0, 1)
-        both_halves((2, 3), 0, 1, 0)
-        quantise_x(0, 2, sca)
-        both_halves((2, 3), 0, 1, 1)
+        quantise_x(0, on_scalar)
+        one_tap((0, 1), 0, 0)
+        quantise_x(2, on_scalar)
+        one_tap((2, 3), 2, 0)
+        one_tap((0, 1), 0, 1)
+        quantise_x(4, on_scalar)
+        one_tap((2, 3), 2, 1)
+
         quantise_w2(0)
-        quantise_x(0, 3, sca)
-        close_half(0, 0, 0, 0)
-        close_half(2, 0, 1, 0)
-        open_taps(0, 0, 2, 0, (0, 1))
-        open_taps(2, 0, 2, 1, (0, 1))
-        quantise_w2(1)
-        for slot, r in ((1, 0), (3, 1)):
-            close_half(slot, 0, r, 1)
-            for i in range(TILES):
-                store(0, r, i)
-        quantise_x(0, 4, vec)
-        close_both((0, 2), 0, 2, sca)
+        close_half(0, 0, 0)
+        quantise_x(6, on_vector)
+        close_half(2, 2, 0)
+        open_half(0, 4, 0)
+        open_half(2, 4, 1)
+        quantise_x(7, on_vector)
 
-        quantise_x(1, 0, vec)
-        both_halves((1, 3), 1, 0, 0)
-        quantise_x(1, 1, vec)
-        both_halves((1, 3), 1, 0, 1)
-        both_halves((0, 2), 1, 1, 0)
-        quantise_x(1, 2, vec)
-        quantise_x(1, 3, vec)
-        quantise_x(1, 4, vec)
-        close_both((1, 3), 1, 0, vec)
-        both_halves((0, 2), 1, 1, 1)
-        close_both((0, 2), 1, 1, vec)
+        quantise_w2(1)
+        for slot, c in ((1, 0), (3, 2)):
+            close_half(slot, c, 1)
+            for i in range(TILES):
+                store(c, i)
+        quantise_x(8, on_vector)
+        close_both((0, 2), 4, on_scalar)
+
+        quantise_x(1, on_vector)
+        one_tap((1, 3), 1, 0)
+        quantise_x(3, on_vector)
+        one_tap((1, 3), 1, 1)
+        one_tap((0, 2), 3, 0)
+        quantise_x(5, on_vector)
+        quantise_x(9, on_vector)
+        close_both((1, 3), 1, on_scalar)
+        one_tap((0, 2), 3, 1)
+        close_both((0, 2), 3, on_vector)
+
         for i in range(TILES):
             for tap in range(TAPS):
-                for h in range(2):
-                    tap_pass((1, 3)[h], 1, 2, h, tap, i)
-            for h in range(2):
-                drain((1, 3)[h], 1, 2, h, i, (sca, vec)[h])
-            store(1, 2, i)
+                for h in range(HALVES):
+                    tap_pass((1, 3)[h], 5, h, tap, i)
+            for h in range(HALVES):
+                drain((1, 3)[h], 5, h, i, (on_scalar, on_vector)[h])
+            store(5, i)

from contextlib import ExitStack

import concourse.mybir as mybir

D, K, M, T = 512, 512, 1024, 1536
FLOPS = 2 * 3 * K * M * T

F32 = mybir.dt.float32
BF16 = mybir.dt.bfloat16
I32 = mybir.dt.int32
U32 = mybir.dt.uint32
U8 = mybir.dt.uint8
FP8X4 = mybir.dt.float8_e4m3fn_x4
FP4X4 = mybir.dt.float4_e2m1fn_x4

P = 128
PACK = 4
QUADRANT = 32
ROWS = 128
COLS = 512
CHUNK = 256
TILES = CHUNK // ROWS
HALVES = M // COLS
TAPS = 3
SLOTS = 4
RUN = 4
PLANE_ROW = (0, 4, 0)


def tile_mix_dconv_tm_none_kernel(tc, x, w0_words, w0_scales, w1_words, w1_scales, w2, out):
    nc = tc.nc
    on_vector, on_scalar = nc.vector.tensor_copy, nc.scalar.copy

    with ExitStack() as ctx:
        keep = ctx.enter_context(tc.tile_pool(name="keep", bufs=1))
        psum = ctx.enter_context(tc.psum_pool(name="psum", bufs=1))
        ctx.enter_context(tc.manual_schedule())

        x_codes = keep.tile([P, T + 2 * D], U32, align_bytes=64)
        x_plane = keep.tile([P, T + 2 * D], U8, align_bytes=64)
        w2_codes = keep.tile([P, M], U32, align_bytes=64)
        w2_plane = keep.tile([P, M], U8, align_bytes=64)
        w1_codes = keep.tile([P, M], U32, align_bytes=64)
        w1_plane = keep.tile([P, M], U8, align_bytes=64)
        w0_codes = keep.tile([P, 2 * M], U8, align_bytes=64)
        w0_plane = keep.tile([P, M], U8, align_bytes=64)
        banks = [[psum.tile([ROWS, COLS], F32, name=f"bank_{s}_{i}") for i in range(TILES)] for s in range(SLOTS)]
        results = [keep.tile([ROWS, M], F32, name=f"result_{n}") for n in range(T // ROWS)]
        raw_x = {}

        def load_rows(name, source, first, width):
            raw = keep.tile([P, PACK, width], F32, name=f"raw_{name}_{first}")
            nc.sync.dma_start(out=raw[:], in_=source[:, first : first + width].rearrange("(p j) w -> p j w", j=PACK))
            return raw

        def load_x(c, chunks):
            raw = load_rows("x", x, c * CHUNK, chunks * CHUNK)
            for u in range(chunks):
                raw_x[c + u] = (raw, c * CHUNK)

        def load_scales(scales, plane, first_row):
            for r in range(4):
                nc.sync.dma_start(
                    out=plane[first_row + r : P : QUADRANT, :].bitcast(I32), in_=scales[0, r:16:4, :].bitcast(I32)
                )

        def quantise(name, raw, codes, plane, first, pieces):
            grouped = []
            for lo, hi, copy in pieces:
                g = keep.tile([P, hi - lo, PACK], BF16, name=f"grouped_{name}_{first + lo}", align_bytes=64)
                copy(
                    out=g[:].rearrange("p (c i) j -> p c j i", i=RUN),
                    in_=raw[:, :, lo:hi].rearrange("p j (c i) -> p c j i", i=RUN),
                )
                grouped.append(g)
            for (lo, hi, copy), g in zip(pieces, grouped):
                nc.vector.quantize_mx(
                    out=codes[:, first + lo : first + hi].bitcast(FP8X4),
                    scales=plane[:, first + lo : first + hi],
                    in_=g[:].rearrange("p w j -> p (w j)"),
                )

        def quantise_x(c, second_copy):
            raw, first = raw_x[c]
            lo = c * CHUNK - first
            pieces = [(lo, lo + ROWS, on_vector), (lo + ROWS, lo + CHUNK, second_copy)]
            quantise("x", raw, x_codes, x_plane, first, pieces)

        def quantise_w2(h):
            pieces = [(0, 256, on_vector), (256, 384, on_vector), (384, COLS, on_scalar)]
            quantise("w2", raw_w2[h], w2_codes, w2_plane, h * COLS, pieces)

        def tap_pass(slot, c, h, tap, i):
            t0 = c * CHUNK + tap * D + i * ROWS
            n0 = h * COLS
            if tap == 0:
                rhs = w0_codes[:, 2 * n0 : 2 * (n0 + COLS)].bitcast(FP4X4)
            else:
                rhs = (w1_codes, w2_codes)[tap - 1][:, n0 : n0 + COLS].bitcast(FP8X4)
            nc.tensor.matmul_mx(
                out=banks[slot][i][:],
                lhsT=x_codes[:, t0 : t0 + ROWS].bitcast(FP8X4),
                lhsT_scale=x_plane[:, t0 : t0 + ROWS],
                rhs=rhs,
                rhs_scale=(w0_plane, w1_plane, w2_plane)[tap][PLANE_ROW[tap] :, n0 : n0 + COLS],
                start=tap == 0,
                stop=tap == TAPS - 1,
            )

        def drain(slot, c, h, i, copy):
            copy(out=results[TILES * c + i][:, h * COLS : (h + 1) * COLS], in_=banks[slot][i][:])

        def store(c, i):
            n = TILES * c + i
            nc.sync.dma_start(out=out[n * ROWS : (n + 1) * ROWS, :], in_=results[n][:])

        def one_tap(slots, c, tap):
            for i in range(TILES):
                for h in range(HALVES):
                    tap_pass(slots[h], c, h, tap, i)

        def open_half(slot, c, h):
            for i in range(TILES):
                for tap in range(TAPS - 1):
                    tap_pass(slot, c, h, tap, i)

        def close_half(slot, c, h):
            for i in range(TILES):
                tap_pass(slot, c, h, TAPS - 1, i)
                drain(slot, c, h, i, on_scalar)

        def close_both(slots, c, second_copy):
            for i in range(TILES):
                for h in range(HALVES):
                    tap_pass(slots[h], c, h, TAPS - 1, i)
                    drain(slots[h], c, h, i, (on_scalar, second_copy)[h])
                store(c, i)

        nc.vector.memset(w0_plane[:].bitcast(I32), 0)
        nc.vector.memset(w1_plane[:].bitcast(I32), 0)

        load_x(0, 1)
        nc.sync.dma_start(out=w0_codes[:].bitcast(I32), in_=w0_words[0].bitcast(I32))
        load_scales(w0_scales, w0_plane, PLANE_ROW[0])
        nc.sync.dma_start(out=w1_codes[:].bitcast(I32), in_=w1_words[0].rearrange("p n t -> p (n t)").bitcast(I32))
        load_x(2, 1)
        load_x(4, 1)
        load_scales(w1_scales, w1_plane, PLANE_ROW[1])
        raw_w2 = [load_rows("w2", w2, 0, COLS)]
        load_x(6, 2)
        raw_w2.append(load_rows("w2", w2, COLS, COLS))
        load_x(8, 2)
        for c in (1, 3, 5):
            load_x(c, 1)

        quantise_x(0, on_scalar)
        one_tap((0, 1), 0, 0)
        quantise_x(2, on_scalar)
        one_tap((2, 3), 2, 0)
        one_tap((0, 1), 0, 1)
        quantise_x(4, on_scalar)
        one_tap((2, 3), 2, 1)

        quantise_w2(0)
        close_half(0, 0, 0)
        quantise_x(6, on_vector)
        close_half(2, 2, 0)
        open_half(0, 4, 0)
        open_half(2, 4, 1)
        quantise_x(7, on_vector)

        quantise_w2(1)
        for slot, c in ((1, 0), (3, 2)):
            close_half(slot, c, 1)
            for i in range(TILES):
                store(c, i)
        quantise_x(8, on_vector)
        close_both((0, 2), 4, on_scalar)

        quantise_x(1, on_vector)
        one_tap((1, 3), 1, 0)
        quantise_x(3, on_vector)
        one_tap((1, 3), 1, 1)
        one_tap((0, 2), 3, 0)
        quantise_x(5, on_vector)
        quantise_x(9, on_vector)
        close_both((1, 3), 1, on_scalar)
        one_tap((0, 2), 3, 1)
        close_both((0, 2), 3, on_vector)

        for i in range(TILES):
            for tap in range(TAPS):
                for h in range(HALVES):
                    tap_pass((1, 3)[h], 5, h, tap, i)
            for h in range(HALVES):
                drain((1, 3)[h], 5, h, i, (on_scalar, on_vector)[h])
            store(5, i)
